import numpy as np
import ml_dtypes


def mxq(x, axis, fmt="e4m3"):
    dtype, down = {"e4m3": (ml_dtypes.float8_e4m3fn, 7), "e5m2": (ml_dtypes.float8_e5m2, 14)}[fmt]
    v = np.moveaxis(np.asarray(x, np.float32).astype(ml_dtypes.bfloat16).astype(np.float64), axis, -1)
    blocks = v.reshape(v.shape[:-1] + (-1, 32))
    amax = np.abs(blocks).max(-1, keepdims=True)
    byte = np.maximum(np.where(amax > 0, np.frexp(amax)[1] - 1 + 127, 0) - down, 1)
    scale = np.exp2(byte - 127.0)
    codes = (blocks / scale).astype(np.float32).astype(dtype).astype(np.float64)
    return np.moveaxis((codes * scale).reshape(v.shape), -1, axis)


WIDE = False


def mx_kscale(k):
    if not WIDE:
        return np.ones(k)
    levels = np.array([10, -10, 5, -5, 0])
    if k % 512:
        return np.exp2(np.random.permutation(np.resize(levels, k // 32))).repeat(32)
    a = np.empty((k // 512, 16))
    for p in range(k // 512):
        a[p, :8] = np.random.permutation(np.resize(levels, 8))
        for g in range(8):
            far = levels[np.abs(levels - a[p, g]) >= 10]
            a[p, g + 8] = far[np.random.randint(len(far))]
    return np.exp2(a.ravel()).repeat(32)


def f64(x):
    return np.asarray(x).astype(np.float64)


def striped(idx):
    return np.tile(idx.reshape(-1, 16).T, (8, 1)).astype(np.uint16)


def unstriped(offs):
    return offs[:16].T.reshape(-1).astype(np.int64)


E2M1 = np.array([0.0, 0.5, 1.0, 1.5, 2.0, 3.0, 4.0, 6.0, -0.0, -0.5, -1.0, -1.5, -2.0, -3.0, -4.0, -6.0])


def pack_weight(w, fmt):
    k, n = w.shape
    w = f64(np.asarray(w, np.float32).astype(ml_dtypes.bfloat16)).reshape(k // 32, 32, n)
    amax = np.abs(w).max(1)
    if fmt == "e4m3":
        byte = np.frexp(amax)[1] - 1 + 127 - 7
    else:
        mant, ex = np.frexp(amax / 6.0)
        byte = np.where(mant > 0.5, ex, ex - 1) + 127
    byte = np.clip(np.where(amax > 0, byte, 1), 1, 254)
    scaled = (w * np.exp2(127.0 - byte)[:, None, :]).reshape(k, n).astype(np.float32)
    by_word = np.ascontiguousarray(scaled.reshape(k // 512, 128, 4, n).transpose(0, 1, 3, 2))
    if fmt == "e4m3":
        words = by_word.astype(ml_dtypes.float8_e4m3fn).view(np.uint8)
    else:
        c = by_word.astype(ml_dtypes.float4_e2m1fn).view(np.uint8) & 0xF
        words = (c[..., 0::2] | (c[..., 1::2] << 4)).reshape(k // 512, 128, 2 * n)
    return np.ascontiguousarray(words), np.ascontiguousarray(byte.astype(np.uint8).reshape(k // 512, 16, n))


def unpack_weight(words, scales, fmt):
    g, _, n = scales.shape
    words = np.ascontiguousarray(words).reshape(g, 128, n, -1)
    if fmt == "e4m3":
        vals = words.view(ml_dtypes.float8_e4m3fn).astype(np.float64)
    else:
        nib = np.empty((g, 128, n, 4), np.uint8)
        nib[..., 0::2] = words & 0xF
        nib[..., 1::2] = words >> 4
        vals = E2M1[nib]
    vals = vals * np.repeat(np.exp2(scales.astype(np.float64) - 127.0), 8, axis=1)[..., None]
    return vals.transpose(0, 1, 3, 2).reshape(g * 512, n)


K, M, T, S = 1024, 1024, 4096, 2048


def setup_inputs():
    n = np.random.standard_normal
    s = mx_kscale(K)[:, None]
    v = pack_weight(n((K, T)) * s, "e4m3")
    return {
        "tab_words": v[0],
        "tab_scales": v[1],
        "w": (n((K, M)) / np.sqrt(K) / s).astype(np.float32),
        "rT": n((M, T)).astype(np.float32),
        "offs": striped(np.random.permutation(T)[:S]),
    }


def reference(tab_words, tab_scales, w, rT, offs):
    tab_ = unpack_weight(tab_words, tab_scales, "e4m3")[:, unstriped(offs)]
    w_ = mxq(f64(w), 0, "e4m3")
    y = w_.T @ tab_
    return (y) + f64(rT)[:, unstriped(offs)]

@@ -1,0 +1,138 @@
+from contextlib import ExitStack
+
+import concourse.mybir as mybir
+
+K, M, T, S = 1024, 1024, 4096, 2048
+FLOPS = 2 * K * M * S
+
+F32 = mybir.dt.float32
+BF16 = mybir.dt.bfloat16
+I32 = mybir.dt.int32
+U32 = mybir.dt.uint32
+U16 = mybir.dt.uint16
+U8 = mybir.dt.uint8
+FP8X4 = mybir.dt.float8_e4m3fn_x4
+ADD = mybir.AluOpType.add
+
+P = 128
+PACK = 4
+K_PASS = P * PACK
+PASSES = K // K_PASS
+ROW_TILES = M // P
+BANK = 512
+W_COLS = 512
+CHUNK = 1024
+LIST_ROWS = 16
+WINDOW_BUFS = 7
+HALF_BUFS = 8
+
+
+def tile_list_tabres_none_kernel(tc, tab_words, tab_scales, w, rT, offs, out):
+    nc = tc.nc
+    with ExitStack() as ctx:
+        keep = ctx.enter_context(tc.tile_pool(name="keep", bufs=1))
+        windows = ctx.enter_context(tc.tile_pool(name="windows", bufs=WINDOW_BUFS))
+        halves = ctx.enter_context(tc.tile_pool(name="halves", bufs=HALF_BUFS))
+        stage = ctx.enter_context(tc.tile_pool(name="stage", bufs=2))
+        products = ctx.enter_context(tc.tile_pool(name="products", bufs=4))
+        psum = ctx.enter_context(tc.psum_pool(name="psum", bufs=8))
+
+        offsets = keep.tile([P, S // LIST_ROWS], U16, name="offsets")
+        nc.sync.dma_start(offsets[:], offs)
+
+        def listed(c0, width):
+            return offsets[:, c0 // LIST_ROWS : (c0 + width) // LIST_ROWS]
+
+        scale_window = keep.tile([P, T], U8, name="scale_window", align_bytes=64)
+        nc.vector.memset(scale_window[:].bitcast(I32), 0)
+        for a in range(PASSES):
+            for q in range(4):
+                row = 32 * q + 4 * a
+                nc.scalar.dma_start(
+                    scale_window[row : row + 4, :].bitcast(I32),
+                    tab_scales[a, 4 * q : 4 * q + 4, :].bitcast(I32),
+                )
+
+        def load_words(a):
+            window = windows.tile([P, T], U32, name=f"words{a}", tag="window")
+            nc.sync.dma_start(window[:].bitcast(I32), tab_words[a].rearrange("p t i -> p (t i)").bitcast(I32))
+            return window
+
+        def load_w(h, a):
+            raw = halves.tile([P, PACK, W_COLS], F32, name=f"w_raw{h}{a}", tag="half")
+            rows = w[a * K_PASS : (a + 1) * K_PASS, h * W_COLS : (h + 1) * W_COLS]
+            nc.sync.dma_start(raw[:], rows.rearrange("(p j) n -> p j n", j=PACK))
+            return raw
+
+        def load_residual(i):
+            window = windows.tile([P, T], F32, name=f"residual{i}", tag="window")
+            nc.sync.dma_start(window[:], rT[i * P : (i + 1) * P, :])
+            return window
+
+        word_windows = [load_words(0)]
+        w_raw = {(0, a): load_w(0, a) for a in range(PASSES)}
+        word_windows.append(load_words(1))
+        residuals = [load_residual(0), load_residual(1)]
+        for a in range(PASSES):
+            w_raw[(1, a)] = load_w(1, a)
+        for i in range(2, WINDOW_BUFS - PASSES):
+            residuals.append(load_residual(i))
+
+        v_scales = keep.tile([P, S], U8, name="v_scales", align_bytes=64)
+        nc.vector.tensor_copy(v_scales[:], scale_window[:].indirect(offsets[:]))
+        v_words = [keep.tile([P, S], U32, name=f"v_words{a}", align_bytes=64) for a in range(PASSES)]
+
+        def gather_words(a):
+            for c0 in range(0, S, CHUNK):
+                nc.vector.tensor_copy(v_words[a][:, c0 : c0 + CHUNK], word_windows[a][:].indirect(listed(c0, CHUNK)))
+
+        w_codes, w_scales = {}, {}
+
+        def quantize_w(h):
+            for a in range(PASSES):
+                grouped = stage.tile([P, W_COLS, PACK], BF16, name="grouped", align_bytes=64)
+                nc.scalar.copy(grouped[:], w_raw[(h, a)][:].rearrange("p j n -> p n j"))
+                w_codes[(h, a)] = keep.tile([P, W_COLS], U32, name=f"w_codes{h}{a}", align_bytes=64)
+                w_scales[(h, a)] = keep.tile([P, W_COLS], U8, name=f"w_scales{h}{a}", align_bytes=64)
+                nc.vector.quantize_mx(
+                    out=w_codes[(h, a)][:].bitcast(FP8X4),
+                    scales=w_scales[(h, a)][:],
+                    in_=grouped[:].rearrange("p n j -> p (n j)"),
+                )
+
+        gather_words(0)
+        quantize_w(0)
+        gather_words(1)
+        for i in range(len(residuals), ROW_TILES - 1):
+            residuals.append(load_residual(i))
+
+        for i in range(ROW_TILES):
+            if i == 1:
+                residuals.append(load_residual(ROW_TILES - 1))
+            if i == 2:
+                quantize_w(1)
+            h, m0 = divmod(i * P, W_COLS)
+            result = halves.tile([P, S], F32, name=f"result{i}", tag="half")
+            for c0 in range(0, S, CHUNK):
+                y = products.tile([P, CHUNK], F32, name="y")
+                for b0 in range(0, CHUNK, BANK):
+                    cols = slice(c0 + b0, c0 + b0 + BANK)
+                    acc = psum.tile([P, BANK], F32, name="acc")
+                    for a in range(PASSES):
+                        nc.tensor.matmul_mx(
+                            out=acc[:],
+                            lhsT=w_codes[(h, a)][:, m0 : m0 + P].bitcast(FP8X4),
+                            lhsT_scale=w_scales[(h, a)][:, m0 : m0 + P],
+                            rhs=v_words[a][:, cols].bitcast(FP8X4),
+                            rhs_scale=v_scales[4 * a : P, cols],
+                            start=(a == 0),
+                            stop=(a == PASSES - 1),
+                        )
+                    nc.scalar.copy(y[:, b0 : b0 + BANK], acc[:])
+                nc.vector.tensor_tensor(
+                    result[:, c0 : c0 + CHUNK], residuals[i][:].indirect(listed(c0, CHUNK)), y[:], ADD
+                )
+                if i == ROW_TILES - 1:
+                    nc.sync.dma_start(out[i * P : (i + 1) * P, c0 : c0 + CHUNK], result[:, c0 : c0 + CHUNK])
+            if i < ROW_TILES - 1:
+                nc.sync.dma_start(out[i * P : (i + 1) * P, :], result[:])

@@ -20,11 +20,13 @@ K_PASS = P * PACK
 PASSES = K // K_PASS
 ROW_TILES = M // P
 BANK = 512
-W_COLS = 512
+W_COLS = 256
 CHUNK = 1024
 LIST_ROWS = 16
+QUADRANT = 32
+SCALE_ROWS = 4
 WINDOW_BUFS = 7
-HALF_BUFS = 8
+STORE_GROUPS = (4, 2, 1, 1)
 
 
 def tile_list_tabres_none_kernel(tc, tab_words, tab_scales, w, rT, offs, out):
@@ -32,36 +34,18 @@ def tile_list_tabres_none_kernel(tc, tab_words, tab_scales, w, rT, offs, out):
     with ExitStack() as ctx:
         keep = ctx.enter_context(tc.tile_pool(name="keep", bufs=1))
         windows = ctx.enter_context(tc.tile_pool(name="windows", bufs=WINDOW_BUFS))
-        halves = ctx.enter_context(tc.tile_pool(name="halves", bufs=HALF_BUFS))
-        stage = ctx.enter_context(tc.tile_pool(name="stage", bufs=2))
+        stage = ctx.enter_context(tc.tile_pool(name="stage", bufs=3))
         products = ctx.enter_context(tc.tile_pool(name="products", bufs=4))
         psum = ctx.enter_context(tc.psum_pool(name="psum", bufs=8))
-
-        offsets = keep.tile([P, S // LIST_ROWS], U16, name="offsets")
-        nc.sync.dma_start(offsets[:], offs)
-
-        def listed(c0, width):
-            return offsets[:, c0 // LIST_ROWS : (c0 + width) // LIST_ROWS]
-
-        scale_window = keep.tile([P, T], U8, name="scale_window", align_bytes=64)
-        nc.vector.memset(scale_window[:].bitcast(I32), 0)
-        for a in range(PASSES):
-            for q in range(4):
-                row = 32 * q + 4 * a
-                nc.scalar.dma_start(
-                    scale_window[row : row + 4, :].bitcast(I32),
-                    tab_scales[a, 4 * q : 4 * q + 4, :].bitcast(I32),
-                )
 
         def load_words(a):
             window = windows.tile([P, T], U32, name=f"words{a}", tag="window")
             nc.sync.dma_start(window[:].bitcast(I32), tab_words[a].rearrange("p t i -> p (t i)").bitcast(I32))
             return window
 
-        def load_w(h, a):
-            raw = halves.tile([P, PACK, W_COLS], F32, name=f"w_raw{h}{a}", tag="half")
-            rows = w[a * K_PASS : (a + 1) * K_PASS, h * W_COLS : (h + 1) * W_COLS]
-            nc.sync.dma_start(raw[:], rows.rearrange("(p j) n -> p j n", j=PACK))
+        def load_w(a):
+            raw = windows.tile([P, PACK, M], F32, name=f"w_raw{a}", tag="window")
+            nc.sync.dma_start(raw[:], w[a * K_PASS : (a + 1) * K_PASS, :].rearrange("(p j) n -> p j n", j=PACK))
             return raw
 
         def load_residual(i):
@@ -70,28 +54,39 @@ def tile_list_tabres_none_kernel(tc, tab_words, tab_scales, w, rT, offs, out):
             return window
 
         word_windows = [load_words(0)]
-        w_raw = {(0, a): load_w(0, a) for a in range(PASSES)}
-        word_windows.append(load_words(1))
-        residuals = [load_residual(0), load_residual(1)]
-        for a in range(PASSES):
-            w_raw[(1, a)] = load_w(1, a)
-        for i in range(2, WINDOW_BUFS - PASSES):
-            residuals.append(load_residual(i))
+        offsets = keep.tile([P, S // LIST_ROWS], U16, name="offsets")
+        nc.sync.dma_start(offsets[:], offs)
 
+        def listed(c0):
+            return offsets[:, c0 // LIST_ROWS : (c0 + CHUNK) // LIST_ROWS]
+
+        scale_window = keep.tile([P, T], U8, name="scale_window", align_bytes=64)
+        nc.vector.memset(scale_window[:].bitcast(I32), 0)
+        for r in range(SCALE_ROWS):
+            for a in range(PASSES):
+                nc.scalar.dma_start(
+                    scale_window[SCALE_ROWS * a + r : P : QUADRANT, :].bitcast(I32),
+                    tab_scales[a, r::SCALE_ROWS, :].bitcast(I32),
+                )
+
+        word_windows.append(load_words(1))
+        w_raw = [load_w(a) for a in range(PASSES)]
+        residuals = [load_residual(i) for i in range(WINDOW_BUFS - 2 * PASSES)]
+
+        v_words = [keep.tile([P, S], U32, name=f"v_words{a}", align_bytes=64) for a in range(PASSES)]
+        for a in range(PASSES):
+            for c0 in range(0, S, CHUNK):
+                nc.vector.tensor_copy(v_words[a][:, c0 : c0 + CHUNK], word_windows[a][:].indirect(listed(c0)))
+            residuals.append(load_residual(len(residuals)))
         v_scales = keep.tile([P, S], U8, name="v_scales", align_bytes=64)
         nc.vector.tensor_copy(v_scales[:], scale_window[:].indirect(offsets[:]))
-        v_words = [keep.tile([P, S], U32, name=f"v_words{a}", align_bytes=64) for a in range(PASSES)]
-
-        def gather_words(a):
-            for c0 in range(0, S, CHUNK):
-                nc.vector.tensor_copy(v_words[a][:, c0 : c0 + CHUNK], word_windows[a][:].indirect(listed(c0, CHUNK)))
 
         w_codes, w_scales = {}, {}
 
         def quantize_w(h):
             for a in range(PASSES):
-                grouped = stage.tile([P, W_COLS, PACK], BF16, name="grouped", align_bytes=64)
-                nc.scalar.copy(grouped[:], w_raw[(h, a)][:].rearrange("p j n -> p n j"))
+                grouped = stage.tile([P, W_COLS, PACK], BF16, name=f"grouped{a}", align_bytes=64)
+                nc.scalar.copy(grouped[:], w_raw[a][:, :, h * W_COLS : (h + 1) * W_COLS].rearrange("p j n -> p n j"))
                 w_codes[(h, a)] = keep.tile([P, W_COLS], U32, name=f"w_codes{h}{a}", align_bytes=64)
                 w_scales[(h, a)] = keep.tile([P, W_COLS], U8, name=f"w_scales{h}{a}", align_bytes=64)
                 nc.vector.quantize_mx(
@@ -100,39 +95,34 @@ def tile_list_tabres_none_kernel(tc, tab_words, tab_scales, w, rT, offs, out):
                     in_=grouped[:].rearrange("p n j -> p (n j)"),
                 )
 
-        gather_words(0)
         quantize_w(0)
-        gather_words(1)
-        for i in range(len(residuals), ROW_TILES - 1):
-            residuals.append(load_residual(i))
-
-        for i in range(ROW_TILES):
-            if i == 1:
-                residuals.append(load_residual(ROW_TILES - 1))
-            if i == 2:
-                quantize_w(1)
-            h, m0 = divmod(i * P, W_COLS)
-            result = halves.tile([P, S], F32, name=f"result{i}", tag="half")
-            for c0 in range(0, S, CHUNK):
-                y = products.tile([P, CHUNK], F32, name="y")
-                for b0 in range(0, CHUNK, BANK):
-                    cols = slice(c0 + b0, c0 + b0 + BANK)
-                    acc = psum.tile([P, BANK], F32, name="acc")
-                    for a in range(PASSES):
-                        nc.tensor.matmul_mx(
-                            out=acc[:],
-                            lhsT=w_codes[(h, a)][:, m0 : m0 + P].bitcast(FP8X4),
-                            lhsT_scale=w_scales[(h, a)][:, m0 : m0 + P],
-                            rhs=v_words[a][:, cols].bitcast(FP8X4),
-                            rhs_scale=v_scales[4 * a : P, cols],
-                            start=(a == 0),
-                            stop=(a == PASSES - 1),
-                        )
-                    nc.scalar.copy(y[:, b0 : b0 + BANK], acc[:])
-                nc.vector.tensor_tensor(
-                    result[:, c0 : c0 + CHUNK], residuals[i][:].indirect(listed(c0, CHUNK)), y[:], ADD
-                )
-                if i == ROW_TILES - 1:
-                    nc.sync.dma_start(out[i * P : (i + 1) * P, c0 : c0 + CHUNK], result[:, c0 : c0 + CHUNK])
-            if i < ROW_TILES - 1:
-                nc.sync.dma_start(out[i * P : (i + 1) * P, :], result[:])
+        i = 0
+        for group in STORE_GROUPS:
+            first = i
+            result = keep.tile([P, group, S], F32, name=f"result{first}")
+            for g in range(group):
+                i = first + g
+                h, m0 = divmod(i * P, W_COLS)
+                if m0 > 0 and (h + 1) * W_COLS < M:
+                    quantize_w(h + 1)
+                if i > 0 and len(residuals) < ROW_TILES:
+                    residuals.append(load_residual(len(residuals)))
+                for c0 in range(0, S, CHUNK):
+                    y = products.tile([P, CHUNK], F32, name="y")
+                    for b0 in range(0, CHUNK, BANK):
+                        cols = slice(c0 + b0, c0 + b0 + BANK)
+                        acc = psum.tile([P, BANK], F32, name="acc")
+                        for a in range(PASSES):
+                            nc.tensor.matmul_mx(
+                                out=acc[:],
+                                lhsT=w_codes[(h, a)][:, m0 : m0 + P].bitcast(FP8X4),
+                                lhsT_scale=w_scales[(h, a)][:, m0 : m0 + P],
+                                rhs=v_words[a][:, cols].bitcast(FP8X4),
+                                rhs_scale=v_scales[SCALE_ROWS * a : P, cols],
+                                start=(a == 0),
+                                stop=(a == PASSES - 1),
+                            )
+                        nc.scalar.copy(y[:, b0 : b0 + BANK], acc[:])
+                    nc.vector.tensor_tensor(result[:, g, c0 : c0 + CHUNK], residuals[i][:].indirect(listed(c0)), y[:], ADD)
+            i = first + group
+            nc.sync.dma_start(out[first * P : i * P, :].rearrange("(g p) s -> p g s", p=P), result[:])

from contextlib import ExitStack

import concourse.mybir as mybir

K, M, T, S = 1024, 1024, 4096, 2048
FLOPS = 2 * K * M * S

F32 = mybir.dt.float32
BF16 = mybir.dt.bfloat16
I32 = mybir.dt.int32
U32 = mybir.dt.uint32
U16 = mybir.dt.uint16
U8 = mybir.dt.uint8
FP8X4 = mybir.dt.float8_e4m3fn_x4
ADD = mybir.AluOpType.add

P = 128
PACK = 4
K_PASS = P * PACK
PASSES = K // K_PASS
ROW_TILES = M // P
BANK = 512
W_COLS = 256
CHUNK = 1024
LIST_ROWS = 16
QUADRANT = 32
SCALE_ROWS = 4
WINDOW_BUFS = 7
STORE_GROUPS = (4, 2, 1, 1)


def tile_list_tabres_none_kernel(tc, tab_words, tab_scales, w, rT, offs, out):
    nc = tc.nc
    with ExitStack() as ctx:
        keep = ctx.enter_context(tc.tile_pool(name="keep", bufs=1))
        windows = ctx.enter_context(tc.tile_pool(name="windows", bufs=WINDOW_BUFS))
        stage = ctx.enter_context(tc.tile_pool(name="stage", bufs=3))
        products = ctx.enter_context(tc.tile_pool(name="products", bufs=4))
        psum = ctx.enter_context(tc.psum_pool(name="psum", bufs=8))

        def load_words(a):
            window = windows.tile([P, T], U32, name=f"words{a}", tag="window")
            nc.sync.dma_start(window[:].bitcast(I32), tab_words[a].rearrange("p t i -> p (t i)").bitcast(I32))
            return window

        def load_w(a):
            raw = windows.tile([P, PACK, M], F32, name=f"w_raw{a}", tag="window")
            nc.sync.dma_start(raw[:], w[a * K_PASS : (a + 1) * K_PASS, :].rearrange("(p j) n -> p j n", j=PACK))
            return raw

        def load_residual(i):
            window = windows.tile([P, T], F32, name=f"residual{i}", tag="window")
            nc.sync.dma_start(window[:], rT[i * P : (i + 1) * P, :])
            return window

        word_windows = [load_words(0)]
        offsets = keep.tile([P, S // LIST_ROWS], U16, name="offsets")
        nc.sync.dma_start(offsets[:], offs)

        def listed(c0):
            return offsets[:, c0 // LIST_ROWS : (c0 + CHUNK) // LIST_ROWS]

        scale_window = keep.tile([P, T], U8, name="scale_window", align_bytes=64)
        nc.vector.memset(scale_window[:].bitcast(I32), 0)
        for r in range(SCALE_ROWS):
            for a in range(PASSES):
                nc.scalar.dma_start(
                    scale_window[SCALE_ROWS * a + r : P : QUADRANT, :].bitcast(I32),
                    tab_scales[a, r::SCALE_ROWS, :].bitcast(I32),
                )

        word_windows.append(load_words(1))
        w_raw = [load_w(a) for a in range(PASSES)]
        residuals = [load_residual(i) for i in range(WINDOW_BUFS - 2 * PASSES)]

        v_words = [keep.tile([P, S], U32, name=f"v_words{a}", align_bytes=64) for a in range(PASSES)]
        for a in range(PASSES):
            for c0 in range(0, S, CHUNK):
                nc.vector.tensor_copy(v_words[a][:, c0 : c0 + CHUNK], word_windows[a][:].indirect(listed(c0)))
            residuals.append(load_residual(len(residuals)))
        v_scales = keep.tile([P, S], U8, name="v_scales", align_bytes=64)
        nc.vector.tensor_copy(v_scales[:], scale_window[:].indirect(offsets[:]))

        w_codes, w_scales = {}, {}

        def quantize_w(h):
            for a in range(PASSES):
                grouped = stage.tile([P, W_COLS, PACK], BF16, name=f"grouped{a}", align_bytes=64)
                nc.scalar.copy(grouped[:], w_raw[a][:, :, h * W_COLS : (h + 1) * W_COLS].rearrange("p j n -> p n j"))
                w_codes[(h, a)] = keep.tile([P, W_COLS], U32, name=f"w_codes{h}{a}", align_bytes=64)
                w_scales[(h, a)] = keep.tile([P, W_COLS], U8, name=f"w_scales{h}{a}", align_bytes=64)
                nc.vector.quantize_mx(
                    out=w_codes[(h, a)][:].bitcast(FP8X4),
                    scales=w_scales[(h, a)][:],
                    in_=grouped[:].rearrange("p n j -> p (n j)"),
                )

        quantize_w(0)
        i = 0
        for group in STORE_GROUPS:
            first = i
            result = keep.tile([P, group, S], F32, name=f"result{first}")
            for g in range(group):
                i = first + g
                h, m0 = divmod(i * P, W_COLS)
                if m0 > 0 and (h + 1) * W_COLS < M:
                    quantize_w(h + 1)
                if i > 0 and len(residuals) < ROW_TILES:
                    residuals.append(load_residual(len(residuals)))
                for c0 in range(0, S, CHUNK):
                    y = products.tile([P, CHUNK], F32, name="y")
                    for b0 in range(0, CHUNK, BANK):
                        cols = slice(c0 + b0, c0 + b0 + BANK)
                        acc = psum.tile([P, BANK], F32, name="acc")
                        for a in range(PASSES):
                            nc.tensor.matmul_mx(
                                out=acc[:],
                                lhsT=w_codes[(h, a)][:, m0 : m0 + P].bitcast(FP8X4),
                                lhsT_scale=w_scales[(h, a)][:, m0 : m0 + P],
                                rhs=v_words[a][:, cols].bitcast(FP8X4),
                                rhs_scale=v_scales[SCALE_ROWS * a : P, cols],
                                start=(a == 0),
                                stop=(a == PASSES - 1),
                            )
                        nc.scalar.copy(y[:, b0 : b0 + BANK], acc[:])
                    nc.vector.tensor_tensor(result[:, g, c0 : c0 + CHUNK], residuals[i][:].indirect(listed(c0)), y[:], ADD)
            i = first + group
            nc.sync.dma_start(out[first * P : i * P, :].rearrange("(g p) s -> p g s", p=P), result[:])
